import numpy as np
import ml_dtypes


def mxq(x, axis, fmt="e4m3"):
    dtype, down = {"e4m3": (ml_dtypes.float8_e4m3fn, 7), "e5m2": (ml_dtypes.float8_e5m2, 14)}[fmt]
    v = np.moveaxis(np.asarray(x, np.float32).astype(ml_dtypes.bfloat16).astype(np.float64), axis, -1)
    blocks = v.reshape(v.shape[:-1] + (-1, 32))
    amax = np.abs(blocks).max(-1, keepdims=True)
    byte = np.maximum(np.where(amax > 0, np.frexp(amax)[1] - 1 + 127, 0) - down, 1)
    scale = np.exp2(byte - 127.0)
    codes = (blocks / scale).astype(np.float32).astype(dtype).astype(np.float64)
    return np.moveaxis((codes * scale).reshape(v.shape), -1, axis)


WIDE = False


def mx_kscale(k):
    if not WIDE:
        return np.ones(k)
    levels = np.array([10, -10, 5, -5, 0])
    if k % 512:
        return np.exp2(np.random.permutation(np.resize(levels, k // 32))).repeat(32)
    a = np.empty((k // 512, 16))
    for p in range(k // 512):
        a[p, :8] = np.random.permutation(np.resize(levels, 8))
        for g in range(8):
            far = levels[np.abs(levels - a[p, g]) >= 10]
            a[p, g + 8] = far[np.random.randint(len(far))]
    return np.exp2(a.ravel()).repeat(32)


def f64(x):
    return np.asarray(x).astype(np.float64)


def striped(idx):
    return np.tile(np.asarray(idx).reshape(-1, 16).T, (8, 1)).astype(np.uint16)


def unstriped(offs):
    return offs[:16].T.reshape(-1).astype(np.int64)


E2M1 = np.array([0.0, 0.5, 1.0, 1.5, 2.0, 3.0, 4.0, 6.0, -0.0, -0.5, -1.0, -1.5, -2.0, -3.0, -4.0, -6.0])


def pack_weight(w, fmt):
    k, n = w.shape
    w = f64(np.asarray(w, np.float32).astype(ml_dtypes.bfloat16)).reshape(k // 32, 32, n)
    amax = np.abs(w).max(1)
    if fmt == "e4m3":
        byte = np.frexp(amax)[1] - 1 + 127 - 7
    else:
        mant, ex = np.frexp(amax / 6.0)
        byte = np.where(mant > 0.5, ex, ex - 1) + 127
    byte = np.clip(np.where(amax > 0, byte, 1), 1, 254)
    scaled = (w * np.exp2(127.0 - byte)[:, None, :]).reshape(k, n).astype(np.float32)
    by_word = np.ascontiguousarray(scaled.reshape(k // 512, 128, 4, n).transpose(0, 1, 3, 2))
    if fmt == "e4m3":
        words = by_word.astype(ml_dtypes.float8_e4m3fn).view(np.uint8)
    else:
        c = by_word.astype(ml_dtypes.float4_e2m1fn).view(np.uint8) & 0xF
        words = (c[..., 0::2] | (c[..., 1::2] << 4)).reshape(k // 512, 128, 2 * n)
    return np.ascontiguousarray(words), np.ascontiguousarray(byte.astype(np.uint8).reshape(k // 512, 16, n))


def unpack_weight(words, scales, fmt):
    g, _, n = scales.shape
    words = np.ascontiguousarray(words).reshape(g, 128, n, -1)
    if fmt == "e4m3":
        vals = words.view(ml_dtypes.float8_e4m3fn).astype(np.float64)
    else:
        nib = np.empty((g, 128, n, 4), np.uint8)
        nib[..., 0::2] = words & 0xF
        nib[..., 1::2] = words >> 4
        vals = E2M1[nib]
    vals = vals * np.repeat(np.exp2(scales.astype(np.float64) - 127.0), 8, axis=1)[..., None]
    return vals.transpose(0, 1, 3, 2).reshape(g * 512, n)


def softplus(v):
    return np.log(1.0 + np.exp(v))


def sigmoid(v):
    return 1.0 / (1.0 + np.exp(-v))


K, R, F, T, J, G = 512, 128, 512, 2048, 512, 128


def setup_inputs():
    n = np.random.standard_normal
    idx = np.random.permutation(T)[:J]
    fk = mx_kscale(K)
    ff = mx_kscale(F)
    tabp = pack_weight(n((K, T)) / fk[:, None], "e4m3")
    dtabp = pack_weight(n((K, T)) / fk[:, None], "e4m3")
    return {
        "tab_words": tabp[0],
        "tab_scales": tabp[1],
        "w1": (n((K, R)) * 1 / np.sqrt(K) * fk[:, None]).astype(np.float32),
        "floor": (np.random.uniform(0.2, 0.8, (R, 1))).astype(np.float32),
        "wo": (n((F, R)) * 1 / np.sqrt(F) * ff[:, None]).astype(np.float32),
        "dy": (n((F, G)) / ff[:, None]).astype(np.float32),
        "dtab_words": dtabp[0],
        "dtab_scales": dtabp[1],
        "og": (np.random.uniform(0.7, 2.0, (R, 1))).astype(np.float32),
        "base": (0.3 * n((R, J))).astype(np.float32),
        "offs": striped(idx),
    }


def reference(tab_words, tab_scales, w1, floor, wo, dy, dtab_words, dtab_scales, og, base, offs):
    idx = unstriped(offs)
    tabu = unpack_weight(tab_words, tab_scales, "e4m3")
    dtabu = unpack_weight(dtab_words, dtab_scales, "e4m3")
    w1q = mxq(f64(w1), 0, "e4m3")
    tabidxg = tabu[:, idx]
    a = w1q.T @ tabidxg
    dtabidxg = dtabu[:, idx]
    ta = w1q.T @ dtabidxg
    h0 = softplus(a)
    h1 = np.log(h0 + f64(floor))
    m1 = h1.reshape(R, G, J // G).mean(axis=2)
    u1 = np.tanh(np.exp(m1))
    woq = mxq(f64(wo), 0, "e4m3")
    dyq = mxq(f64(dy), 0, "e4m3")
    c0 = woq.T @ dyq
    dm1 = c0 * (1.0 - np.square(u1)) * np.exp(m1)
    e1 = dm1 / 4.0
    r1 = np.repeat(e1, J // G, axis=1)
    dh0 = r1 / (h0 + f64(floor))
    xh0 = ta * sigmoid(a)
    xh1 = xh0 / (h0 + f64(floor))
    xm1 = xh1.reshape(R, G, J // G).mean(axis=2)
    xu1 = xm1 * np.exp(m1) * (1.0 - np.square(u1))
    xdm1 = xu1 * u1 * 2.0 * (-1.0) * c0 * np.exp(m1) + xm1 * np.exp(m1) * c0 * (1.0 - np.square(u1))
    xe1 = xdm1 / 4.0
    xr1 = np.repeat(xe1, J // G, axis=1)
    xdh0 = (xr1 - xh0 * r1 / (h0 + f64(floor))) / (h0 + f64(floor))
    xda = xdh0 * sigmoid(a) + ta * sigmoid(a) * (1.0 - sigmoid(a)) * dh0
    y = xda * f64(og) + f64(base)
    return y

@@ -1,0 +1,180 @@
+from contextlib import ExitStack
+
+import concourse.mybir as mybir
+
+K, R, F, T, J, G = 512, 128, 512, 2048, 512, 128
+FLOPS = 2 * K * R * J * 2 + 2 * F * R * G
+
+F32 = mybir.dt.float32
+BF16 = mybir.dt.bfloat16
+I32 = mybir.dt.int32
+U32 = mybir.dt.uint32
+U16 = mybir.dt.uint16
+U8 = mybir.dt.uint8
+FP8X4 = mybir.dt.float8_e4m3fn_x4
+ACT = mybir.ActivationFunctionType
+ALU = mybir.AluOpType
+AX = mybir.AxisListType
+
+P = 128
+PACK = 4
+POOL = J // G
+HALVES = 2
+JH = J // HALVES
+GH = G // HALVES
+DTAB_ROW = 4
+TINY = 2.0**-62
+
+
+def tile_attend_hvcgeometricpool_kernel(tc, tab_words, tab_scales, w1, floor, wo, dy, dtab_words, dtab_scales, og, base, offs, out):
+    nc = tc.nc
+    with ExitStack() as ctx:
+        sb = ctx.enter_context(tc.tile_pool(name="sb", bufs=1))
+        ps = ctx.enter_context(tc.psum_pool(name="ps", bufs=1))
+
+        def halves(name, dtype=F32):
+            return [sb.tile([P, JH], dtype, name="%s%d" % (name, h), align_bytes=64) for h in range(HALVES)]
+
+        def banks(name):
+            return [ps.tile([P, JH], F32, name="%s%d" % (name, h)) for h in range(HALVES)]
+
+        offsets = sb.tile([P, J // 16], U16, name="offsets")
+        tab_s = sb.tile([P, T], U8, name="tab_s", tag="s_tabs")
+        dtab_s = sb.tile([P, T], U8, name="dtab_s")
+        w1_raw = sb.tile([P, PACK, R], F32, name="w1_raw", tag="s_w1")
+        one = sb.tile([P, 1], F32, name="one", tag="s_tabw")
+        tiny = sb.tile([P, 1], F32, name="tiny")
+        warm = sb.tile([P, 1], F32, name="warm", tag="s_warm")
+
+        nc.vector.memset(tab_s[:].bitcast(I32), 0)
+        nc.vector.memset(one[:], 1.0)
+        nc.vector.tensor_scalar(tiny[:], one[:], TINY, None, ALU.mult)
+        nc.vector.memset(dtab_s[:].bitcast(I32), 0)
+        nc.scalar.activation(warm[:], tiny[:], ACT.Sigmoid)
+
+        nc.sync.dma_start(offsets[:], offs)
+        nc.sync.dma_start(w1_raw[:], w1.rearrange("(p j) r -> p j r", j=PACK))
+        for f in range(4):
+            nc.sync.dma_start(tab_s[f:P:32, :].bitcast(I32), tab_scales[0, f:16:4, :].bitcast(I32))
+        tab_w = sb.tile([P, T], U32, name="tab_w", tag="s_tabw")
+        nc.sync.dma_start(tab_w[:].bitcast(I32), tab_words[0].rearrange("p n t -> p (n t)").bitcast(I32))
+        for f in range(4):
+            nc.sync.dma_start(dtab_s[DTAB_ROW + f : P : 32, :].bitcast(I32), dtab_scales[0, f:16:4, :].bitcast(I32))
+        dtab_w = sb.tile([P, T], U32, name="dtab_w", tag="s_warm")
+        nc.sync.dma_start(dtab_w[:].bitcast(I32), dtab_words[0].rearrange("p n t -> p (n t)").bitcast(I32))
+
+        w1_bf = sb.tile([P, R, PACK], BF16, name="w1_bf", tag="s_w1bf", align_bytes=64)
+        w1_q = sb.tile([P, R], U32, name="w1_q", align_bytes=64)
+        w1_s = sb.tile([P, R], U8, name="w1_s", align_bytes=64)
+        nc.scalar.copy(w1_bf[:], w1_raw[:].rearrange("p j r -> p r j"))
+        g_tab_s = sb.tile([P, J], U8, name="g_tab_s", align_bytes=64)
+        nc.vector.tensor_copy(g_tab_s[:], tab_s[:].indirect(offsets[:]))
+        nc.vector.quantize_mx(w1_q[:].bitcast(FP8X4), w1_s[:], w1_bf[:].rearrange("p r j -> p (r j)"))
+        wo_raw = sb.tile([P, PACK, R], F32, name="wo_raw", tag="s_w1")
+        nc.sync.dma_start(wo_raw[:], wo.rearrange("(p j) r -> p j r", j=PACK))
+        dy_raw = sb.tile([P, PACK, G], F32, name="dy_raw", tag="s_tabs")
+        nc.sync.dma_start(dy_raw[:], dy.rearrange("(p j) g -> p j g", j=PACK))
+        floor_sb = sb.tile([P, 1], F32, name="floor_sb", tag="s_w1bf", align_bytes=64)
+        nc.sync.dma_start(floor_sb[:], floor)
+
+        cols = [slice(h * JH, (h + 1) * JH) for h in range(HALVES)]
+        grps = [slice(h * GH, (h + 1) * GH) for h in range(HALVES)]
+        lists = [offsets[:, h * JH // 16 : (h + 1) * JH // 16] for h in range(HALVES)]
+
+        g_tab_w = [sb.tile([P, JH], U32, name="g_tab_w%d" % h, tag="s_gtab%d" % h, align_bytes=64) for h in range(HALVES)]
+        a = banks("a")
+        t = halves("t")
+        for h in range(HALVES):
+            nc.vector.tensor_copy(g_tab_w[h][:], tab_w[:].indirect(lists[h]))
+            nc.tensor.matmul_mx(a[h][:], lhsT=w1_q[:].bitcast(FP8X4), lhsT_scale=w1_s[:], rhs=g_tab_w[h][:].bitcast(FP8X4), rhs_scale=g_tab_s[:, cols[h]], start=True, stop=True)
+            nc.scalar.activation(t[h][:], a[h][:], ACT.Sigmoid, scale=-1.0)
+
+        og_sb = sb.tile([P, 1], F32, name="og_sb", tag="s_gtab0", align_bytes=64)
+        nc.sync.dma_start(og_sb[:], og)
+        base_sb = sb.tile([P, J], F32, name="base_sb", tag="s_tabw")
+        nc.sync.dma_start(base_sb[:], base)
+
+        g_dtab_s = sb.tile([P, J], U8, name="g_dtab_s", align_bytes=64)
+        nc.vector.tensor_copy(g_dtab_s[:], dtab_s[:].indirect(offsets[:]))
+        g_dtab_w = halves("g_dtab_w", U32)
+        ta = banks("ta")
+        for h in range(HALVES):
+            nc.vector.tensor_copy(g_dtab_w[h][:], dtab_w[:].indirect(lists[h]))
+            nc.tensor.matmul_mx(ta[h][:], lhsT=w1_q[:].bitcast(FP8X4), lhsT_scale=w1_s[:], rhs=g_dtab_w[h][:].bitcast(FP8X4), rhs_scale=g_dtab_s[DTAB_ROW:P, cols[h]], start=True, stop=True)
+
+        last_bf = sb.tile([P, R + G, PACK], BF16, name="last_bf", align_bytes=64)
+        last_q = sb.tile([P, R + G], U32, name="last_q", align_bytes=64)
+        last_s = sb.tile([P, R + G], U8, name="last_s", align_bytes=64)
+        nc.gpsimd.tensor_scalar(last_bf[:, 0:R, :], wo_raw[:].rearrange("p j r -> p r j"), 1.0, 0.0, ALU.mult, ALU.add)
+        nc.gpsimd.tensor_scalar(last_bf[:, R : R + G, :], dy_raw[:].rearrange("p j g -> p g j"), 1.0, 0.0, ALU.mult, ALU.add)
+
+        def by_group(x):
+            return x.rearrange("p (g i) -> p g i", i=POOL)
+
+        def spread(x, h):
+            return x[:, grps[h]].unsqueeze(2).to_broadcast([P, GH, POOL])
+
+        ln_t = halves("ln_t")
+        soft = halves("soft")
+        h1 = halves("h1")
+        ln_s = halves("ln_s")
+        ln_q = halves("ln_q")
+        y = halves("y")
+        m_sum = sb.tile([P, G], F32, name="m_sum")
+        for h in range(HALVES):
+            nc.scalar.activation(ln_t[h][:], t[h][:], ACT.Ln, bias=tiny[:])
+        for h in range(HALVES):
+            nc.vector.scalar_tensor_tensor(soft[h][:], ln_t[h][:], -1.0, a[h][:], ALU.mult, ALU.max)
+        for h in range(HALVES):
+            nc.scalar.activation(h1[h][:], soft[h][:], ACT.Ln, bias=floor_sb[:])
+        for h in range(HALVES):
+            nc.vector.tensor_tensor(ln_s[h][:], a[h][:], soft[h][:], ALU.subtract)
+        for h in range(HALVES):
+            nc.gpsimd.tensor_tensor(ln_q[h][:], ln_s[h][:], h1[h][:], ALU.subtract)
+            nc.vector.tensor_reduce(m_sum[:, grps[h]], by_group(h1[h][:]), AX.X, ALU.add)
+        nc.vector.quantize_mx(last_q[:].bitcast(FP8X4), last_s[:], last_bf[:].rearrange("p c j -> p (c j)"))
+        c0 = ps.tile([P, G], F32, name="c0")
+        nc.tensor.matmul_mx(c0[:], lhsT=last_q[:, 0:R].bitcast(FP8X4), lhsT_scale=last_s[:, 0:R], rhs=last_q[:, R : R + G].bitcast(FP8X4), rhs_scale=last_s[:, R : R + G], start=True, stop=True)
+        for h in range(HALVES):
+            nc.vector.tensor_tensor(y[h][:], ta[h][:], t[h][:], ALU.mult)
+
+        q = halves("q")
+        pool_e = sb.tile([P, G], F32, name="pool_e")
+        u = sb.tile([P, G], F32, name="u")
+        u2 = sb.tile([P, G], F32, name="u2")
+        nc.scalar.activation(pool_e[:], m_sum[:], ACT.Exp, scale=1.0 / POOL)
+        nc.scalar.activation(q[0][:], ln_q[0][:], ACT.Exp)
+        nc.scalar.activation(u[:], pool_e[:], ACT.Tanh)
+        nc.scalar.activation(q[1][:], ln_q[1][:], ACT.Exp)
+        nc.scalar.activation(u2[:], u[:], ACT.Square, scale=0.5)
+
+        p = halves("p")
+        p_sum = sb.tile([P, G], F32, name="p_sum")
+        c_e = sb.tile([P, G], F32, name="c_e")
+        u_e = sb.tile([P, G], F32, name="u_e")
+        a_n = sb.tile([P, G], F32, name="a_n")
+        b_n = sb.tile([P, G], F32, name="b_n")
+        z = halves("z")
+        zb = halves("zb")
+        d = halves("d")
+        x = halves("x")
+        res = halves("res")
+
+        nc.vector.scalar_tensor_tensor(c_e[:], c0[:], og_sb[:], pool_e[:], ALU.mult, ALU.mult)
+        nc.vector.tensor_tensor(p[0][:], ta[0][:], q[0][:], ALU.mult)
+        nc.vector.tensor_tensor(u_e[:], u[:], pool_e[:], ALU.mult)
+        nc.vector.tensor_tensor(p[1][:], ta[1][:], q[1][:], ALU.mult)
+        nc.vector.scalar_tensor_tensor(a_n[:], u2[:], 0.25, c_e[:], ALU.subtract, ALU.mult)
+        for h in range(HALVES):
+            nc.vector.tensor_reduce(p_sum[:, grps[h]], by_group(p[h][:]), AX.X, ALU.add)
+        nc.vector.tensor_tensor(z[0][:], p[0][:], y[0][:], ALU.subtract)
+        nc.vector.scalar_tensor_tensor(b_n[:], u_e[:], 0.5, p_sum[:], ALU.subtract, ALU.mult)
+        nc.vector.tensor_tensor(z[1][:], p[1][:], y[1][:], ALU.subtract)
+        for h in range(HALVES):
+            nc.vector.tensor_tensor(by_group(d[h][:]), by_group(q[h][:]), spread(a_n, h), ALU.mult)
+            nc.vector.scalar_tensor_tensor(by_group(zb[h][:]), spread(b_n, h), 0.5, by_group(z[h][:]), ALU.mult, ALU.add)
+        for h in range(HALVES):
+            nc.vector.tensor_tensor(x[h][:], zb[h][:], d[h][:], ALU.mult)
+        for h in range(HALVES):
+            nc.vector.tensor_tensor(res[h][:], x[h][:], base_sb[:, cols[h]], ALU.add)
+            nc.sync.dma_start(out[:, cols[h]], res[h][:])

@@ -42,12 +42,12 @@ def tile_attend_hvcgeometricpool_kernel(tc, tab_words, tab_scales, w1, floor, wo
         tab_s = sb.tile([P, T], U8, name="tab_s", tag="s_tabs")
         dtab_s = sb.tile([P, T], U8, name="dtab_s")
         w1_raw = sb.tile([P, PACK, R], F32, name="w1_raw", tag="s_w1")
-        one = sb.tile([P, 1], F32, name="one", tag="s_tabw")
+        one = sb.tile([P, 1], F32, name="one", tag="s_tabw", align_bytes=64)
         tiny = sb.tile([P, 1], F32, name="tiny")
         warm = sb.tile([P, 1], F32, name="warm", tag="s_warm")
 
         nc.vector.memset(tab_s[:].bitcast(I32), 0)
-        nc.vector.memset(one[:], 1.0)
+        nc.gpsimd.memset(one[:], 1.0)
         nc.vector.tensor_scalar(tiny[:], one[:], TINY, None, ALU.mult)
         nc.vector.memset(dtab_s[:].bitcast(I32), 0)
         nc.scalar.activation(warm[:], tiny[:], ACT.Sigmoid)
@@ -56,32 +56,34 @@ def tile_attend_hvcgeometricpool_kernel(tc, tab_words, tab_scales, w1, floor, wo
         nc.sync.dma_start(w1_raw[:], w1.rearrange("(p j) r -> p j r", j=PACK))
         for f in range(4):
             nc.sync.dma_start(tab_s[f:P:32, :].bitcast(I32), tab_scales[0, f:16:4, :].bitcast(I32))
-        tab_w = sb.tile([P, T], U32, name="tab_w", tag="s_tabw")
+        tab_w = sb.tile([P, T], U32, name="tab_w", tag="s_tabw", align_bytes=64)
         nc.sync.dma_start(tab_w[:].bitcast(I32), tab_words[0].rearrange("p n t -> p (n t)").bitcast(I32))
-        for f in range(4):
-            nc.sync.dma_start(dtab_s[DTAB_ROW + f : P : 32, :].bitcast(I32), dtab_scales[0, f:16:4, :].bitcast(I32))
         dtab_w = sb.tile([P, T], U32, name="dtab_w", tag="s_warm")
         nc.sync.dma_start(dtab_w[:].bitcast(I32), dtab_words[0].rearrange("p n t -> p (n t)").bitcast(I32))
 
-        w1_bf = sb.tile([P, R, PACK], BF16, name="w1_bf", tag="s_w1bf", align_bytes=64)
+        floor_sb = sb.tile([P, 1], F32, name="floor_sb")
+        og_sb = sb.tile([P, 1], F32, name="og_sb")
+        nc.gpsimd.dma_start(floor_sb[:], floor)
+        nc.gpsimd.dma_start(og_sb[:], og)
+        w1_bf = sb.tile([P, R, PACK], BF16, name="w1_bf", align_bytes=64)
         w1_q = sb.tile([P, R], U32, name="w1_q", align_bytes=64)
         w1_s = sb.tile([P, R], U8, name="w1_s", align_bytes=64)
         nc.scalar.copy(w1_bf[:], w1_raw[:].rearrange("p j r -> p r j"))
-        g_tab_s = sb.tile([P, J], U8, name="g_tab_s", align_bytes=64)
+        for f in range(4):
+            nc.scalar.dma_start(dtab_s[DTAB_ROW + f : P : 32, :].bitcast(I32), dtab_scales[0, f:16:4, :].bitcast(I32))
+        g_tab_s = sb.tile([P, J], U8, name="g_tab_s", tag="s_gtabs", align_bytes=64)
         nc.vector.tensor_copy(g_tab_s[:], tab_s[:].indirect(offsets[:]))
         nc.vector.quantize_mx(w1_q[:].bitcast(FP8X4), w1_s[:], w1_bf[:].rearrange("p r j -> p (r j)"))
         wo_raw = sb.tile([P, PACK, R], F32, name="wo_raw", tag="s_w1")
         nc.sync.dma_start(wo_raw[:], wo.rearrange("(p j) r -> p j r", j=PACK))
         dy_raw = sb.tile([P, PACK, G], F32, name="dy_raw", tag="s_tabs")
         nc.sync.dma_start(dy_raw[:], dy.rearrange("(p j) g -> p j g", j=PACK))
-        floor_sb = sb.tile([P, 1], F32, name="floor_sb", tag="s_w1bf", align_bytes=64)
-        nc.sync.dma_start(floor_sb[:], floor)
 
         cols = [slice(h * JH, (h + 1) * JH) for h in range(HALVES)]
         grps = [slice(h * GH, (h + 1) * GH) for h in range(HALVES)]
         lists = [offsets[:, h * JH // 16 : (h + 1) * JH // 16] for h in range(HALVES)]
 
-        g_tab_w = [sb.tile([P, JH], U32, name="g_tab_w%d" % h, tag="s_gtab%d" % h, align_bytes=64) for h in range(HALVES)]
+        g_tab_w = halves("g_tab_w", U32)
         a = banks("a")
         t = halves("t")
         for h in range(HALVES):
@@ -89,12 +91,10 @@ def tile_attend_hvcgeometricpool_kernel(tc, tab_words, tab_scales, w1, floor, wo
             nc.tensor.matmul_mx(a[h][:], lhsT=w1_q[:].bitcast(FP8X4), lhsT_scale=w1_s[:], rhs=g_tab_w[h][:].bitcast(FP8X4), rhs_scale=g_tab_s[:, cols[h]], start=True, stop=True)
             nc.scalar.activation(t[h][:], a[h][:], ACT.Sigmoid, scale=-1.0)
 
-        og_sb = sb.tile([P, 1], F32, name="og_sb", tag="s_gtab0", align_bytes=64)
-        nc.sync.dma_start(og_sb[:], og)
-        base_sb = sb.tile([P, J], F32, name="base_sb", tag="s_tabw")
+        base_sb = sb.tile([P, J], F32, name="base_sb", tag="s_gtabs", align_bytes=64)
         nc.sync.dma_start(base_sb[:], base)
 
-        g_dtab_s = sb.tile([P, J], U8, name="g_dtab_s", align_bytes=64)
+        g_dtab_s = sb.tile([P, J], U8, name="g_dtab_s", tag="s_tabw", align_bytes=64)
         nc.vector.tensor_copy(g_dtab_s[:], dtab_s[:].indirect(offsets[:]))
         g_dtab_w = halves("g_dtab_w", U32)
         ta = banks("ta")
@@ -115,23 +115,28 @@ def tile_attend_hvcgeometricpool_kernel(tc, tab_words, tab_scales, w1, floor, wo
             return x[:, grps[h]].unsqueeze(2).to_broadcast([P, GH, POOL])
 
         ln_t = halves("ln_t")
-        soft = halves("soft")
+        soft_all = sb.tile([P, J], F32, name="soft_all", tag="s_warm")
+        soft = [soft_all[:, c] for c in cols]
         h1 = halves("h1")
         ln_s = halves("ln_s")
-        ln_q = halves("ln_q")
         y = halves("y")
         m_sum = sb.tile([P, G], F32, name="m_sum")
-        for h in range(HALVES):
-            nc.scalar.activation(ln_t[h][:], t[h][:], ACT.Ln, bias=tiny[:])
-        for h in range(HALVES):
-            nc.vector.scalar_tensor_tensor(soft[h][:], ln_t[h][:], -1.0, a[h][:], ALU.mult, ALU.max)
-        for h in range(HALVES):
-            nc.scalar.activation(h1[h][:], soft[h][:], ACT.Ln, bias=floor_sb[:])
+        quarters = [(h, slice(c, c + JH // 2)) for h in range(HALVES) for c in (0, JH // 2)]
+        for h, c in quarters:
+            nc.scalar.activation(ln_t[h][:, c], t[h][:, c], ACT.Ln, bias=tiny[:])
+        for h, c in quarters:
+            nc.vector.scalar_tensor_tensor(soft[h][:, c], ln_t[h][:, c], -1.0, a[h][:, c], ALU.mult, ALU.max)
+        for h, c in quarters:
+            nc.scalar.activation(h1[h][:, c], soft[h][:, c], ACT.Ln, bias=floor_sb[:])
+        warm_exp = sb.tile([P, 1], F32, name="warm_exp")
+        nc.scalar.activation(warm_exp[:], h1[HALVES - 1][:, JH - 1 : JH], ACT.Exp)
         for h in range(HALVES):
             nc.vector.tensor_tensor(ln_s[h][:], a[h][:], soft[h][:], ALU.subtract)
         for h in range(HALVES):
-            nc.gpsimd.tensor_tensor(ln_q[h][:], ln_s[h][:], h1[h][:], ALU.subtract)
             nc.vector.tensor_reduce(m_sum[:, grps[h]], by_group(h1[h][:]), AX.X, ALU.add)
+        ln_q = [sb.tile([P, JH], F32, name="ln_q0", tag="s_tabs"), sb.tile([P, JH], F32, name="ln_q1")]
+        for h in range(HALVES):
+            nc.gpsimd.tensor_tensor(ln_q[h][:], ln_s[h][:], h1[h][:], ALU.subtract)
         nc.vector.quantize_mx(last_q[:].bitcast(FP8X4), last_s[:], last_bf[:].rearrange("p c j -> p (c j)"))
         c0 = ps.tile([P, G], F32, name="c0")
         nc.tensor.matmul_mx(c0[:], lhsT=last_q[:, 0:R].bitcast(FP8X4), lhsT_scale=last_s[:, 0:R], rhs=last_q[:, R : R + G].bitcast(FP8X4), rhs_scale=last_s[:, R : R + G], start=True, stop=True)
@@ -142,10 +147,10 @@ def tile_attend_hvcgeometricpool_kernel(tc, tab_words, tab_scales, w1, floor, wo
         pool_e = sb.tile([P, G], F32, name="pool_e")
         u = sb.tile([P, G], F32, name="u")
         u2 = sb.tile([P, G], F32, name="u2")
-        nc.scalar.activation(pool_e[:], m_sum[:], ACT.Exp, scale=1.0 / POOL)
         nc.scalar.activation(q[0][:], ln_q[0][:], ACT.Exp)
-        nc.scalar.activation(u[:], pool_e[:], ACT.Tanh)
+        nc.scalar.activation(pool_e[:], m_sum[:], ACT.Exp, scale=1.0 / POOL)
         nc.scalar.activation(q[1][:], ln_q[1][:], ACT.Exp)
+        nc.scalar.activation(u[:], pool_e[:], ACT.Tanh)
         nc.scalar.activation(u2[:], u[:], ACT.Square, scale=0.5)
 
         p = halves("p")
@@ -160,13 +165,13 @@ def tile_attend_hvcgeometricpool_kernel(tc, tab_words, tab_scales, w1, floor, wo
         x = halves("x")
         res = halves("res")
 
-        nc.vector.scalar_tensor_tensor(c_e[:], c0[:], og_sb[:], pool_e[:], ALU.mult, ALU.mult)
         nc.vector.tensor_tensor(p[0][:], ta[0][:], q[0][:], ALU.mult)
-        nc.vector.tensor_tensor(u_e[:], u[:], pool_e[:], ALU.mult)
+        nc.vector.scalar_tensor_tensor(c_e[:], c0[:], og_sb[:], pool_e[:], ALU.mult, ALU.mult)
         nc.vector.tensor_tensor(p[1][:], ta[1][:], q[1][:], ALU.mult)
-        nc.vector.scalar_tensor_tensor(a_n[:], u2[:], 0.25, c_e[:], ALU.subtract, ALU.mult)
         for h in range(HALVES):
             nc.vector.tensor_reduce(p_sum[:, grps[h]], by_group(p[h][:]), AX.X, ALU.add)
+        nc.vector.tensor_tensor(u_e[:], u[:], pool_e[:], ALU.mult)
+        nc.vector.scalar_tensor_tensor(a_n[:], u2[:], 0.25, c_e[:], ALU.subtract, ALU.mult)
         nc.vector.tensor_tensor(z[0][:], p[0][:], y[0][:], ALU.subtract)
         nc.vector.scalar_tensor_tensor(b_n[:], u_e[:], 0.5, p_sum[:], ALU.subtract, ALU.mult)
         nc.vector.tensor_tensor(z[1][:], p[1][:], y[1][:], ALU.subtract)

from contextlib import ExitStack

import concourse.mybir as mybir

K, R, F, T, J, G = 512, 128, 512, 2048, 512, 128
FLOPS = 2 * K * R * J * 2 + 2 * F * R * G

F32 = mybir.dt.float32
BF16 = mybir.dt.bfloat16
I32 = mybir.dt.int32
U32 = mybir.dt.uint32
U16 = mybir.dt.uint16
U8 = mybir.dt.uint8
FP8X4 = mybir.dt.float8_e4m3fn_x4
ACT = mybir.ActivationFunctionType
ALU = mybir.AluOpType
AX = mybir.AxisListType

P = 128
PACK = 4
POOL = J // G
HALVES = 2
JH = J // HALVES
GH = G // HALVES
DTAB_ROW = 4
TINY = 2.0**-62


def tile_attend_hvcgeometricpool_kernel(tc, tab_words, tab_scales, w1, floor, wo, dy, dtab_words, dtab_scales, og, base, offs, out):
    nc = tc.nc
    with ExitStack() as ctx:
        sb = ctx.enter_context(tc.tile_pool(name="sb", bufs=1))
        ps = ctx.enter_context(tc.psum_pool(name="ps", bufs=1))

        def halves(name, dtype=F32):
            return [sb.tile([P, JH], dtype, name="%s%d" % (name, h), align_bytes=64) for h in range(HALVES)]

        def banks(name):
            return [ps.tile([P, JH], F32, name="%s%d" % (name, h)) for h in range(HALVES)]

        offsets = sb.tile([P, J // 16], U16, name="offsets")
        tab_s = sb.tile([P, T], U8, name="tab_s", tag="s_tabs")
        dtab_s = sb.tile([P, T], U8, name="dtab_s")
        w1_raw = sb.tile([P, PACK, R], F32, name="w1_raw", tag="s_w1")
        one = sb.tile([P, 1], F32, name="one", tag="s_tabw", align_bytes=64)
        tiny = sb.tile([P, 1], F32, name="tiny")
        warm = sb.tile([P, 1], F32, name="warm", tag="s_warm")

        nc.vector.memset(tab_s[:].bitcast(I32), 0)
        nc.gpsimd.memset(one[:], 1.0)
        nc.vector.tensor_scalar(tiny[:], one[:], TINY, None, ALU.mult)
        nc.vector.memset(dtab_s[:].bitcast(I32), 0)
        nc.scalar.activation(warm[:], tiny[:], ACT.Sigmoid)

        nc.sync.dma_start(offsets[:], offs)
        nc.sync.dma_start(w1_raw[:], w1.rearrange("(p j) r -> p j r", j=PACK))
        for f in range(4):
            nc.sync.dma_start(tab_s[f:P:32, :].bitcast(I32), tab_scales[0, f:16:4, :].bitcast(I32))
        tab_w = sb.tile([P, T], U32, name="tab_w", tag="s_tabw", align_bytes=64)
        nc.sync.dma_start(tab_w[:].bitcast(I32), tab_words[0].rearrange("p n t -> p (n t)").bitcast(I32))
        dtab_w = sb.tile([P, T], U32, name="dtab_w", tag="s_warm")
        nc.sync.dma_start(dtab_w[:].bitcast(I32), dtab_words[0].rearrange("p n t -> p (n t)").bitcast(I32))

        floor_sb = sb.tile([P, 1], F32, name="floor_sb")
        og_sb = sb.tile([P, 1], F32, name="og_sb")
        nc.gpsimd.dma_start(floor_sb[:], floor)
        nc.gpsimd.dma_start(og_sb[:], og)
        w1_bf = sb.tile([P, R, PACK], BF16, name="w1_bf", align_bytes=64)
        w1_q = sb.tile([P, R], U32, name="w1_q", align_bytes=64)
        w1_s = sb.tile([P, R], U8, name="w1_s", align_bytes=64)
        nc.scalar.copy(w1_bf[:], w1_raw[:].rearrange("p j r -> p r j"))
        for f in range(4):
            nc.scalar.dma_start(dtab_s[DTAB_ROW + f : P : 32, :].bitcast(I32), dtab_scales[0, f:16:4, :].bitcast(I32))
        g_tab_s = sb.tile([P, J], U8, name="g_tab_s", tag="s_gtabs", align_bytes=64)
        nc.vector.tensor_copy(g_tab_s[:], tab_s[:].indirect(offsets[:]))
        nc.vector.quantize_mx(w1_q[:].bitcast(FP8X4), w1_s[:], w1_bf[:].rearrange("p r j -> p (r j)"))
        wo_raw = sb.tile([P, PACK, R], F32, name="wo_raw", tag="s_w1")
        nc.sync.dma_start(wo_raw[:], wo.rearrange("(p j) r -> p j r", j=PACK))
        dy_raw = sb.tile([P, PACK, G], F32, name="dy_raw", tag="s_tabs")
        nc.sync.dma_start(dy_raw[:], dy.rearrange("(p j) g -> p j g", j=PACK))

        cols = [slice(h * JH, (h + 1) * JH) for h in range(HALVES)]
        grps = [slice(h * GH, (h + 1) * GH) for h in range(HALVES)]
        lists = [offsets[:, h * JH // 16 : (h + 1) * JH // 16] for h in range(HALVES)]

        g_tab_w = halves("g_tab_w", U32)
        a = banks("a")
        t = halves("t")
        for h in range(HALVES):
            nc.vector.tensor_copy(g_tab_w[h][:], tab_w[:].indirect(lists[h]))
            nc.tensor.matmul_mx(a[h][:], lhsT=w1_q[:].bitcast(FP8X4), lhsT_scale=w1_s[:], rhs=g_tab_w[h][:].bitcast(FP8X4), rhs_scale=g_tab_s[:, cols[h]], start=True, stop=True)
            nc.scalar.activation(t[h][:], a[h][:], ACT.Sigmoid, scale=-1.0)

        base_sb = sb.tile([P, J], F32, name="base_sb", tag="s_gtabs", align_bytes=64)
        nc.sync.dma_start(base_sb[:], base)

        g_dtab_s = sb.tile([P, J], U8, name="g_dtab_s", tag="s_tabw", align_bytes=64)
        nc.vector.tensor_copy(g_dtab_s[:], dtab_s[:].indirect(offsets[:]))
        g_dtab_w = halves("g_dtab_w", U32)
        ta = banks("ta")
        for h in range(HALVES):
            nc.vector.tensor_copy(g_dtab_w[h][:], dtab_w[:].indirect(lists[h]))
            nc.tensor.matmul_mx(ta[h][:], lhsT=w1_q[:].bitcast(FP8X4), lhsT_scale=w1_s[:], rhs=g_dtab_w[h][:].bitcast(FP8X4), rhs_scale=g_dtab_s[DTAB_ROW:P, cols[h]], start=True, stop=True)

        last_bf = sb.tile([P, R + G, PACK], BF16, name="last_bf", align_bytes=64)
        last_q = sb.tile([P, R + G], U32, name="last_q", align_bytes=64)
        last_s = sb.tile([P, R + G], U8, name="last_s", align_bytes=64)
        nc.gpsimd.tensor_scalar(last_bf[:, 0:R, :], wo_raw[:].rearrange("p j r -> p r j"), 1.0, 0.0, ALU.mult, ALU.add)
        nc.gpsimd.tensor_scalar(last_bf[:, R : R + G, :], dy_raw[:].rearrange("p j g -> p g j"), 1.0, 0.0, ALU.mult, ALU.add)

        def by_group(x):
            return x.rearrange("p (g i) -> p g i", i=POOL)

        def spread(x, h):
            return x[:, grps[h]].unsqueeze(2).to_broadcast([P, GH, POOL])

        ln_t = halves("ln_t")
        soft_all = sb.tile([P, J], F32, name="soft_all", tag="s_warm")
        soft = [soft_all[:, c] for c in cols]
        h1 = halves("h1")
        ln_s = halves("ln_s")
        y = halves("y")
        m_sum = sb.tile([P, G], F32, name="m_sum")
        quarters = [(h, slice(c, c + JH // 2)) for h in range(HALVES) for c in (0, JH // 2)]
        for h, c in quarters:
            nc.scalar.activation(ln_t[h][:, c], t[h][:, c], ACT.Ln, bias=tiny[:])
        for h, c in quarters:
            nc.vector.scalar_tensor_tensor(soft[h][:, c], ln_t[h][:, c], -1.0, a[h][:, c], ALU.mult, ALU.max)
        for h, c in quarters:
            nc.scalar.activation(h1[h][:, c], soft[h][:, c], ACT.Ln, bias=floor_sb[:])
        warm_exp = sb.tile([P, 1], F32, name="warm_exp")
        nc.scalar.activation(warm_exp[:], h1[HALVES - 1][:, JH - 1 : JH], ACT.Exp)
        for h in range(HALVES):
            nc.vector.tensor_tensor(ln_s[h][:], a[h][:], soft[h][:], ALU.subtract)
        for h in range(HALVES):
            nc.vector.tensor_reduce(m_sum[:, grps[h]], by_group(h1[h][:]), AX.X, ALU.add)
        ln_q = [sb.tile([P, JH], F32, name="ln_q0", tag="s_tabs"), sb.tile([P, JH], F32, name="ln_q1")]
        for h in range(HALVES):
            nc.gpsimd.tensor_tensor(ln_q[h][:], ln_s[h][:], h1[h][:], ALU.subtract)
        nc.vector.quantize_mx(last_q[:].bitcast(FP8X4), last_s[:], last_bf[:].rearrange("p c j -> p (c j)"))
        c0 = ps.tile([P, G], F32, name="c0")
        nc.tensor.matmul_mx(c0[:], lhsT=last_q[:, 0:R].bitcast(FP8X4), lhsT_scale=last_s[:, 0:R], rhs=last_q[:, R : R + G].bitcast(FP8X4), rhs_scale=last_s[:, R : R + G], start=True, stop=True)
        for h in range(HALVES):
            nc.vector.tensor_tensor(y[h][:], ta[h][:], t[h][:], ALU.mult)

        q = halves("q")
        pool_e = sb.tile([P, G], F32, name="pool_e")
        u = sb.tile([P, G], F32, name="u")
        u2 = sb.tile([P, G], F32, name="u2")
        nc.scalar.activation(q[0][:], ln_q[0][:], ACT.Exp)
        nc.scalar.activation(pool_e[:], m_sum[:], ACT.Exp, scale=1.0 / POOL)
        nc.scalar.activation(q[1][:], ln_q[1][:], ACT.Exp)
        nc.scalar.activation(u[:], pool_e[:], ACT.Tanh)
        nc.scalar.activation(u2[:], u[:], ACT.Square, scale=0.5)

        p = halves("p")
        p_sum = sb.tile([P, G], F32, name="p_sum")
        c_e = sb.tile([P, G], F32, name="c_e")
        u_e = sb.tile([P, G], F32, name="u_e")
        a_n = sb.tile([P, G], F32, name="a_n")
        b_n = sb.tile([P, G], F32, name="b_n")
        z = halves("z")
        zb = halves("zb")
        d = halves("d")
        x = halves("x")
        res = halves("res")

        nc.vector.tensor_tensor(p[0][:], ta[0][:], q[0][:], ALU.mult)
        nc.vector.scalar_tensor_tensor(c_e[:], c0[:], og_sb[:], pool_e[:], ALU.mult, ALU.mult)
        nc.vector.tensor_tensor(p[1][:], ta[1][:], q[1][:], ALU.mult)
        for h in range(HALVES):
            nc.vector.tensor_reduce(p_sum[:, grps[h]], by_group(p[h][:]), AX.X, ALU.add)
        nc.vector.tensor_tensor(u_e[:], u[:], pool_e[:], ALU.mult)
        nc.vector.scalar_tensor_tensor(a_n[:], u2[:], 0.25, c_e[:], ALU.subtract, ALU.mult)
        nc.vector.tensor_tensor(z[0][:], p[0][:], y[0][:], ALU.subtract)
        nc.vector.scalar_tensor_tensor(b_n[:], u_e[:], 0.5, p_sum[:], ALU.subtract, ALU.mult)
        nc.vector.tensor_tensor(z[1][:], p[1][:], y[1][:], ALU.subtract)
        for h in range(HALVES):
            nc.vector.tensor_tensor(by_group(d[h][:]), by_group(q[h][:]), spread(a_n, h), ALU.mult)
            nc.vector.scalar_tensor_tensor(by_group(zb[h][:]), spread(b_n, h), 0.5, by_group(z[h][:]), ALU.mult, ALU.add)
        for h in range(HALVES):
            nc.vector.tensor_tensor(x[h][:], zb[h][:], d[h][:], ALU.mult)
        for h in range(HALVES):
            nc.vector.tensor_tensor(res[h][:], x[h][:], base_sb[:, cols[h]], ALU.add)
            nc.sync.dma_start(out[:, cols[h]], res[h][:])
